import numpy as np
import ml_dtypes


def mxq(x, axis, fmt="e4m3"):
    dtype, down = {"e4m3": (ml_dtypes.float8_e4m3fn, 7), "e5m2": (ml_dtypes.float8_e5m2, 14)}[fmt]
    v = np.moveaxis(np.asarray(x, np.float32).astype(ml_dtypes.bfloat16).astype(np.float64), axis, -1)
    blocks = v.reshape(v.shape[:-1] + (-1, 32))
    amax = np.abs(blocks).max(-1, keepdims=True)
    byte = np.maximum(np.where(amax > 0, np.frexp(amax)[1] - 1 + 127, 0) - down, 1)
    scale = np.exp2(byte - 127.0)
    codes = (blocks / scale).astype(np.float32).astype(dtype).astype(np.float64)
    return np.moveaxis((codes * scale).reshape(v.shape), -1, axis)


WIDE = False


def mx_kscale(k):
    if not WIDE:
        return np.ones(k)
    levels = np.array([10, -10, 5, -5, 0])
    if k % 512:
        return np.exp2(np.random.permutation(np.resize(levels, k // 32))).repeat(32)
    a = np.empty((k // 512, 16))
    for p in range(k // 512):
        a[p, :8] = np.random.permutation(np.resize(levels, 8))
        for g in range(8):
            far = levels[np.abs(levels - a[p, g]) >= 10]
            a[p, g + 8] = far[np.random.randint(len(far))]
    return np.exp2(a.ravel()).repeat(32)


def f64(x):
    return np.asarray(x).astype(np.float64)


def striped(idx):
    return np.tile(idx.reshape(-1, 16).T, (8, 1)).astype(np.uint16)


def unstriped(offs):
    return offs[:16].T.reshape(-1).astype(np.int64)


def striped8(idx):
    return np.concatenate([x.reshape(-1, 16).T for x in idx]).astype(np.uint16)


def runs(offs, k):
    lists = np.stack([offs[16 * r : 16 * r + 16].T.reshape(-1) for r in range(8)]).astype(np.int64)
    return lists[np.arange(k) % 512 // 64]


def pack_weight(w):
    k, n = w.shape
    w = f64(np.asarray(w, np.float32).astype(ml_dtypes.bfloat16)).reshape(k // 32, 32, n)
    amax = np.abs(w).max(1)
    byte = np.clip(np.where(amax > 0, np.frexp(amax)[1] - 1 + 127 - 7, 1), 1, 254)
    scaled = (w * np.exp2(127.0 - byte)[:, None, :]).reshape(k, n).astype(np.float32)
    words = np.ascontiguousarray(scaled.reshape(k // 512, 128, 4, n).transpose(0, 1, 3, 2)).astype(ml_dtypes.float8_e4m3fn).view(np.uint8)
    return words, np.ascontiguousarray(byte.astype(np.uint8).reshape(k // 512, 16, n))


def unpack_weight(words, scales):
    g, p, n, _ = words.shape
    vals = np.ascontiguousarray(words).view(ml_dtypes.float8_e4m3fn).astype(np.float64) * np.repeat(np.exp2(scales.astype(np.float64) - 127.0), 8, axis=1)[..., None]
    return vals.transpose(0, 1, 3, 2).reshape(g * 512, n)


E2M1 = np.array([0.0, 0.5, 1.0, 1.5, 2.0, 3.0, 4.0, 6.0, -0.0, -0.5, -1.0, -1.5, -2.0, -3.0, -4.0, -6.0])


def pack_fp4(w):
    k, n = w.shape
    w = f64(np.asarray(w, np.float32).astype(ml_dtypes.bfloat16)).reshape(k // 32, 32, n)
    amax = np.abs(w).max(1)
    mant, ex = np.frexp(amax / 6.0)
    byte = np.clip(np.where(amax > 0, np.where(mant > 0.5, ex, ex - 1) + 127, 1), 1, 254)
    scaled = (w * np.exp2(127.0 - byte)[:, None, :]).reshape(k, n).astype(np.float32)
    c = np.ascontiguousarray(scaled.reshape(k // 512, 128, 4, n).transpose(0, 1, 3, 2)).astype(ml_dtypes.float4_e2m1fn).view(np.uint8) & 0xF
    words = (c[..., 0::2] | (c[..., 1::2] << 4)).reshape(k // 512, 128, 2 * n)
    return np.ascontiguousarray(words), np.ascontiguousarray(byte.astype(np.uint8).reshape(k // 512, 16, n))


def unpack_fp4(words, scales):
    g, _, n = scales.shape
    words = np.ascontiguousarray(words).reshape(g, 128, n, 2)
    nib = np.empty((g, 128, n, 4), np.uint8)
    nib[..., 0::2] = words & 0xF
    nib[..., 1::2] = words >> 4
    vals = E2M1[nib] * np.repeat(np.exp2(scales.astype(np.float64) - 127.0), 8, axis=1)[..., None]
    return vals.transpose(0, 1, 3, 2).reshape(g * 512, n)


def planes(y):
    n, m = y.shape
    v = y.astype(np.float32).astype(ml_dtypes.bfloat16).astype(np.float64).reshape(n // 32, 32, m)
    top = np.abs(v).max(1)
    byte = np.clip(np.where(top > 0, np.frexp(top)[1] - 1 + 127 - 7, 1), 1, 254)
    codes = (v * np.exp2(127.0 - byte)[:, None, :]).reshape(n, m).astype(np.float32).astype(ml_dtypes.float8_e4m3fn).view(np.uint8)
    words = codes.reshape(n // 512, 128, 4, m).transpose(0, 1, 3, 2)
    return np.ascontiguousarray(words), np.ascontiguousarray(byte.astype(np.uint8).reshape(n // 512, 16, m))


K, T, S, N, H = 512, 2048, 512, 512, 512


def setup_inputs():
    n = np.random.standard_normal
    s = mx_kscale(K)[:, None]
    u = mx_kscale(H)
    packed_xT = pack_weight(n((K, T)) * s)
    packed_w1 = pack_fp4(n((K, H)) / np.sqrt(K) / s)
    packed_w2 = pack_fp4(n((K, H)) / np.sqrt(K) / s)
    packed_w3 = pack_fp4(n((H, N)) / np.sqrt(H) / u[:, None])
    return {
        "x_words": packed_xT[0],
        "x_scales": packed_xT[1],
        "w1_words": packed_w1[0],
        "w1_scales": packed_w1[1],
        "w2_words": packed_w2[0],
        "w2_scales": packed_w2[1],
        "gn": (np.random.uniform(0.5, 1.5, (H, 1)) * u[:, None]).astype(np.float32),
        "w3_words": packed_w3[0],
        "w3_scales": packed_w3[1],
        "offs": striped(np.random.permutation(T)[:S]),
        "two": striped(np.random.permutation(T)[:S]),
        "e1": striped8(np.stack([np.random.permutation(S) for _ in range(8)])),
        "e0": striped8(np.stack([np.random.permutation(S) for _ in range(8)])),
        "v0": striped8(np.stack([np.random.permutation(S) for _ in range(8)])),
        "v1": striped8(np.stack([np.random.permutation(S) for _ in range(8)])),
    }


def reference(x_words, x_scales, w1_words, w1_scales, w2_words, w2_scales, gn, w3_words, w3_scales, offs, two, e1, e0, v0, v1):
    x_two = unpack_weight(x_words, x_scales)[:, unstriped(two)]
    c = unpack_fp4(w2_words, w2_scales).T @ x_two
    xq = unpack_weight(x_words, x_scales)[:, unstriped(offs)]
    y = unpack_fp4(w1_words, w1_scales).T @ xq
    t1 = np.clip(0.5 * (y[np.arange(H)[:, None], runs(e1, H)] - (y[np.arange(H)[:, None], runs(e0, H)])) + 0.5, 0.0, 1.0)
    sm = ((t1) ** 2) * (-2.0 * t1 + 3.0)
    z = f64(gn) * (c[np.arange(H)[:, None], runs(v0, H)] + sm * (c[np.arange(H)[:, None], runs(v1, H)] - (c[np.arange(H)[:, None], runs(v0, H)])))
    out_0 = unpack_fp4(w3_words, w3_scales).T @ mxq(z, 0, "e4m3")
    return (out_0,) + planes(out_0)

@@ -1,0 +1,307 @@
+from contextlib import ExitStack
+
+import concourse.mybir as mybir
+from concourse.masks import make_identity
+
+K, T, S, N, H = 512, 2048, 512, 512, 512
+FLOPS = 2 * K * H * S * 2 + 2 * H * N * S
+
+F32 = mybir.dt.float32
+BF16 = mybir.dt.bfloat16
+I32 = mybir.dt.int32
+U32 = mybir.dt.uint32
+U16 = mybir.dt.uint16
+U8 = mybir.dt.uint8
+FP8X4 = mybir.dt.float8_e4m3fn_x4
+FP4X4 = mybir.dt.float4_e2m1fn_x4
+ACT = mybir.ActivationFunctionType
+ALU = mybir.AluOpType
+
+P = 128
+PACK = 4
+LANES = 16
+HALF = S // 2
+BLOCK = 128
+
+
+def tile_picked_smstep_none_po_kernel(
+    tc, x_words, x_scales, w1_words, w1_scales, w2_words, w2_scales, gn, w3_words, w3_scales,
+    offs, two, e1, e0, v0, v1, out_0, out_1, out_2,
+):
+    nc = tc.nc
+    with ExitStack() as ctx:
+        keep = ctx.enter_context(tc.tile_pool(name="keep", bufs=1))
+        psum = ctx.enter_context(tc.psum_pool(name="psum", bufs=1))
+
+        def sb(name, shape, dtype, tag=None):
+            return keep.tile(shape, dtype, name=name, tag=tag or name, align_bytes=64)
+
+        def bank(name, tag):
+            return psum.tile([P, PACK * BLOCK], F32, name=name, tag=tag)
+
+        def load_list(name, src):
+            tile = sb(name, [P, S // LANES], U16)
+            nc.sync.dma_start(tile[:], src)
+            return tile
+
+        def load_scales(queue, tile, src):
+            for q in range(4):
+                queue.dma_start(tile[32 * q : 32 * q + 4, :].bitcast(I32), src[0, 4 * q : 4 * q + 4, :].bitcast(I32))
+
+        def entries(tile, first, count):
+            return tile[:, first // LANES : (first + count) // LANES]
+
+        xw = sb("xw", [P, T], I32)
+        xs = sb("xs", [P, T], U8)
+        raw_s = [sb("raw_s%d" % i, [P, H], U8) for i in range(3)]
+        gain_rows = sb("gain_rows", [P, P], F32)
+        ident = sb("ident", [P, P], F32)
+        warm = sb("warm", [P, 2], F32)
+
+        def load_words(i, src):
+            tile = sb("raw_w%d" % i, [P, 2 * H], U8, tag="raw_w")
+            nc.sync.dma_start(tile[:].bitcast(I32), src[0].bitcast(I32))
+            return tile
+
+        nc.vector.memset(xs[:].bitcast(I32), 0)
+        nc.gpsimd.memset(raw_s[0][:].bitcast(I32), 0)
+        load_scales(nc.gpsimd, raw_s[0], w1_scales)
+        nc.vector.memset(warm[:, 0:1], 0.0)
+        for i in (1, 2):
+            nc.vector.memset(raw_s[i][:].bitcast(I32), 0)
+        make_identity(nc, ident[:])
+        nc.gpsimd.memset(gain_rows[:], 0.0)
+
+        offs_t = load_list("offs_t", offs)
+        two_t = load_list("two_t", two)
+        nc.sync.dma_start(xw[:], x_words[0].rearrange("p n t -> p (n t)").bitcast(I32))
+        load_scales(nc.scalar, xs, x_scales)
+        raw_w = [load_words(0, w1_words)]
+        e0_t = load_list("e0_t", e0)
+        e1_t = load_list("e1_t", e1)
+        load_scales(nc.sync, raw_s[1], w2_scales)
+        nc.sync.dma_start(
+            gain_rows[0:PACK, :].rearrange("t (g r) -> t g r", r=LANES),
+            gn.rearrange("(g t r) o -> t g (r o)", t=PACK, r=LANES),
+        )
+        v0_t = load_list("v0_t", v0)
+        v1_t = load_list("v1_t", v1)
+        load_scales(nc.sync, raw_s[2], w3_scales)
+
+        nc.scalar.activation(warm[:, 1:2], warm[:, 0:1], ACT.Relu)
+
+        pick_s = [sb("pick_s%d" % i, [P, S], U8) for i in range(2)]
+        pick_w = [sb("pick_w%d" % i, [P, S], U32) for i in range(2)]
+        dealt_w = [sb("dealt_w%d" % i, [P, 2 * H], U8) for i in range(3)]
+        dealt_s = [sb("dealt_s%d" % i, [P, H], U8) for i in range(3)]
+
+        def deal_runs(i):
+            for dst, src in ((dealt_w[i], raw_w[i]), (dealt_s[i], raw_s[i])):
+                nc.gpsimd.tensor_copy(
+                    dst[:].bitcast(I32).rearrange("p (t g r) -> p t g r", t=PACK, g=8),
+                    src[:].bitcast(I32).rearrange("p (g t r) -> p t g r", t=PACK, g=8),
+                )
+
+        def project(i, dst, t, first, count):
+            nc.tensor.matmul_mx(
+                dst[:, first : first + count],
+                lhsT=dealt_w[i][:, 2 * P * t : 2 * P * (t + 1)].bitcast(FP4X4),
+                lhsT_scale=dealt_s[i][:, P * t : P * (t + 1)],
+                rhs=pick_w[i][:, first : first + count].bitcast(FP8X4),
+                rhs_scale=pick_s[i][:, first : first + count],
+                start=True,
+                stop=True,
+            )
+
+        nc.vector.tensor_copy(pick_s[0][:], xs[:].indirect(offs_t[:]))
+        nc.vector.tensor_copy(pick_s[1][:], xs[:].indirect(two_t[:]))
+        deal_runs(0)
+        raw_w.append(load_words(1, w2_words))
+        y_ps = [bank("y_ps%d" % t, "proj%d" % t) for t in range(PACK)]
+        for first in (0, HALF):
+            nc.vector.tensor_copy(
+                pick_w[0][:, first : first + HALF], xw[:].bitcast(U32).indirect(entries(offs_t, first, HALF))
+            )
+            for t in range(PACK):
+                project(0, y_ps[t], t, first, HALF)
+        y = [sb("y%d" % t, [P, S], F32) for t in range(PACK)]
+        for t in range(PACK):
+            nc.scalar.copy(y[t][:], y_ps[t][:])
+
+        nc.vector.tensor_copy(pick_w[1][:], xw[:].bitcast(U32).indirect(two_t[:]))
+        deal_runs(1)
+        raw_w.append(load_words(2, w3_words))
+
+        gain_ps = bank("gain_ps", "pairs")
+        nc.tensor.transpose(gain_ps[:, 0:P], gain_rows[:], ident[:])
+        gain = sb("gain", [P, PACK], F32)
+        nc.scalar.copy(gain[:], gain_ps[:, 0:PACK])
+
+        rise, square, share0, share1 = {}, {}, {}, {}
+
+        def flat(tile):
+            return tile[:].rearrange("p t j -> p (t j)")
+
+        def differences(h, u):
+            step = 2 * h + u
+            low = sb("low%d" % step, [P, 2, HALF], F32, tag="work%d" % step)
+            diff = sb("diff%d" % step, [P, 2, HALF], F32)
+            fall = sb("fall%d" % step, [P, 2, HALF], F32)
+            rise[h, u] = sb("rise%d" % step, [P, 2, HALF], F32)
+            square[h, u] = sb("square%d" % step, [P, 2, HALF], F32, tag="work%d" % (step + 2))
+            for i in range(2):
+                nc.vector.tensor_copy(low[:, i, :], y[2 * u + i][:].indirect(entries(e0_t, HALF * h, HALF)))
+            for i in range(2):
+                nc.vector.tensor_tensor(
+                    diff[:, i, :], y[2 * u + i][:].indirect(entries(e1_t, HALF * h, HALF)), low[:, i, :], ALU.subtract
+                )
+            nc.scalar.activation(flat(rise[h, u]), flat(diff), ACT.Relu, bias=1.0)
+            nc.scalar.activation(flat(fall), flat(rise[h, u]), ACT.Relu, bias=2.0, scale=-1.0)
+            nc.scalar.activation(flat(square[h, u]), flat(fall), ACT.Square, scale=0.5)
+
+        def shares(h, u):
+            step = 2 * h + u
+            share0[h, u] = sb("share0_%d" % step, [P, 2, HALF], F32)
+            share1[h, u] = sb("share1_%d" % step, [P, 2, HALF], F32)
+            nc.vector.scalar_tensor_tensor(
+                flat(share0[h, u]), flat(rise[h, u]), 1.0, flat(square[h, u]), ALU.add, ALU.mult
+            )
+            nc.scalar.activation(flat(share1[h, u]), flat(share0[h, u]), ACT.Copy, bias=1.0, scale=-1.0)
+
+        c = [sb("c%d" % t, [P, S], F32) for t in range(PACK)]
+
+        def second_projection(t):
+            c_ps = bank("c_ps%d" % t, "proj%d" % t)
+            project(1, c_ps, t, 0, S)
+            nc.scalar.activation(c[t][:], c_ps[:], ACT.Copy, scale=gain[:, t : t + 1])
+
+        differences(0, 0)
+        second_projection(0)
+        differences(0, 1)
+        shares(0, 0)
+        second_projection(1)
+        differences(1, 0)
+        shares(0, 1)
+        second_projection(2)
+        second_projection(3)
+        differences(1, 1)
+
+        nc.vector.tensor_copy(
+            dealt_w[2][:].rearrange("p (t m b) -> p t m b", t=PACK, b=2),
+            raw_w[2][:].rearrange("p (m t b) -> p t m b", t=PACK, b=2),
+        )
+        nc.vector.tensor_copy(
+            dealt_s[2][:].rearrange("p (t m) -> p t m", t=PACK),
+            raw_s[2][:].rearrange("p (m t) -> p t m", t=PACK),
+        )
+
+        parts = {}
+        blocks = S // BLOCK
+        last = blocks - 1
+
+        def blend(b):
+            first = BLOCK * b
+            h, local = divmod(first, HALF)
+            for t in range(PACK):
+                for i, (lst, share) in enumerate(((v0_t, share0), (v1_t, share1))):
+                    parts[b, t, i] = sb("part%d_%d_%d" % (b, t, i), [P, BLOCK], F32)
+                    nc.vector.tensor_tensor(
+                        parts[b, t, i][:],
+                        c[t][:].indirect(entries(lst, first, BLOCK)),
+                        share[h, t // 2][:, t % 2, local : local + BLOCK],
+                        ALU.mult,
+                    )
+
+        out_codes = sb("out_codes", [P, S], U32)
+        out_scales = sb("out_scales", [P, S], U8)
+        out_rows = out_0.rearrange("(p t) j -> p t j", t=PACK)
+
+        z_packed = {}
+        o_packed = [sb("o_packed%d" % b, [P, BLOCK * PACK], BF16) for b in range(S // BLOCK)]
+
+        def turn(b):
+            z_rows = sb("z_rows%d" % b, [P, H], BF16, tag="z_rows")
+            successor = (b + 2, 0, 0) if b + 2 <= last else (last, PACK - 1, 0)
+            z_packed[b] = sb("z_packed%d" % b, [P, BLOCK * PACK], BF16, tag="part%d_%d_%d" % successor if b < last else None)
+            groups = ((0, PACK),) if b < last else ((0, PACK - 1), (PACK - 1, PACK))
+            for lo, hi in groups:
+                sums = bank("sums%d_%d" % (b, lo), "sums" if lo == 0 else "proj0")
+                for t in range(lo, hi):
+                    for i in range(2):
+                        nc.tensor.matmul(
+                            sums[:, P * t : P * (t + 1)], lhsT=parts[b, t, i][:], rhs=ident[:],
+                            is_transpose=True, start=i == 0, stop=i == 1,
+                        )
+                nc.scalar.copy(
+                    z_rows[:].rearrange("j (g t r) -> j g t r", t=PACK, r=LANES)[:, :, lo:hi, :],
+                    sums[:].rearrange("j (t g r) -> j g t r", t=PACK, r=LANES)[:, :, lo:hi, :],
+                )
+            pairs = bank("pairs%d" % b, "pairs")
+            words = z_rows[:].bitcast(F32)
+            for u in range(2):
+                nc.tensor.transpose(pairs[:, BLOCK * u : BLOCK * (u + 1)], words[:, u : H // 2 : 2], ident[:])
+            nc.scalar.copy(
+                z_packed[b][:].bitcast(F32).rearrange("p (j u) -> p j u", u=2),
+                pairs[:, 0 : 2 * BLOCK].rearrange("p (u j) -> p j u", u=2),
+            )
+
+        def layer(b):
+            cols = slice(BLOCK * b, BLOCK * (b + 1))
+            z_codes = sb("z_codes%d" % b, [P, BLOCK], U32)
+            z_scales = sb("z_scales%d" % b, [P, BLOCK], U8)
+            nc.vector.quantize_mx(z_codes[:].bitcast(FP8X4), z_scales[:], z_packed[b][:])
+            result = sb("result%d" % b, [P, PACK, BLOCK], F32)
+            packed = o_packed[b][:].rearrange("p (j t) -> p j t", t=PACK)
+            groups = ((0, PACK),) if b < last else ((0, 2), (2, PACK))
+            for lo, hi in groups:
+                acc = bank("acc%d_%d" % (b, lo), "acc%d" % (b % 2) if lo == 0 else "proj1")
+                for t in range(lo, hi):
+                    nc.tensor.matmul_mx(
+                        acc[:, BLOCK * t : BLOCK * (t + 1)],
+                        lhsT=dealt_w[2][:, 2 * P * t : 2 * P * (t + 1)].bitcast(FP4X4),
+                        lhsT_scale=dealt_s[2][:, P * t : P * (t + 1)],
+                        rhs=z_codes[:].bitcast(FP8X4),
+                        rhs_scale=z_scales[:],
+                        start=True,
+                        stop=True,
+                    )
+                if b < last - 1:
+                    nc.scalar.copy(packed, acc[:].rearrange("p (t j) -> p j t", t=PACK))
+                copy = nc.vector.tensor_copy if (b == last - 1 or lo > 0) else nc.scalar.copy
+                copy(result[:, lo:hi, :].rearrange("p t j -> p (t j)"), acc[:, BLOCK * lo : BLOCK * hi])
+                nc.sync.dma_start(out_rows[:, lo:hi, cols], result[:, lo:hi, :])
+            if b >= last - 1:
+                nc.vector.tensor_copy(packed, result[:].rearrange("p t j -> p j t"))
+
+        def planes(b):
+            cols = slice(BLOCK * b, BLOCK * (b + 1))
+            nc.vector.quantize_mx(out_codes[:, cols].bitcast(FP8X4), out_scales[:, cols], o_packed[b][:])
+
+        out_words = out_1[0].rearrange("p n t -> p (n t)").bitcast(I32)
+
+        blend(0)
+        shares(1, 0)
+        turn(0)
+        blend(1)
+        shares(1, 1)
+        turn(1)
+        layer(0)
+        blend(2)
+        turn(2)
+        layer(1)
+        layer(2)
+        blend(3)
+        turn(3)
+        planes(0)
+        planes(1)
+        planes(2)
+        nc.sync.dma_start(out_words[:, 0 : BLOCK * last], out_codes[:, 0 : BLOCK * last].bitcast(I32))
+        layer(3)
+        planes(3)
+
+        nc.scalar.dma_start(out_words[:, BLOCK * last : S], out_codes[:, BLOCK * last : S].bitcast(I32))
+        for q in range(4):
+            queue = nc.scalar if q % 2 else nc.sync
+            queue.dma_start(
+                out_2[0, 4 * q : 4 * q + 4, :].bitcast(I32), out_scales[32 * q : 32 * q + 4, :].bitcast(I32)
+            )

@@ -20,8 +20,13 @@ ALU = mybir.AluOpType
 P = 128
 PACK = 4
 LANES = 16
+RUNS = P // LANES
+QUADRANTS = 4
 HALF = S // 2
 BLOCK = 128
+BLOCKS = S // BLOCK
+LAST = BLOCKS - 1
+LEAD = 2
 
 
 def tile_picked_smstep_none_po_kernel(
@@ -33,275 +38,275 @@ def tile_picked_smstep_none_po_kernel(
         keep = ctx.enter_context(tc.tile_pool(name="keep", bufs=1))
         psum = ctx.enter_context(tc.psum_pool(name="psum", bufs=1))
 
-        def sb(name, shape, dtype, tag=None):
+        def sbuf(name, shape, dtype, tag=None):
             return keep.tile(shape, dtype, name=name, tag=tag or name, align_bytes=64)
 
         def bank(name, tag):
             return psum.tile([P, PACK * BLOCK], F32, name=name, tag=tag)
 
         def load_list(name, src):
-            tile = sb(name, [P, S // LANES], U16)
+            tile = sbuf(name, [P, S // LANES], U16)
             nc.sync.dma_start(tile[:], src)
             return tile
 
+        def scale_rows(tile, q):
+            return tile[32 * q : 32 * q + PACK, :].bitcast(I32)
+
         def load_scales(queue, tile, src):
-            for q in range(4):
-                queue.dma_start(tile[32 * q : 32 * q + 4, :].bitcast(I32), src[0, 4 * q : 4 * q + 4, :].bitcast(I32))
+            for q in range(QUADRANTS):
+                queue.dma_start(scale_rows(tile, q), src[0, PACK * q : PACK * (q + 1), :].bitcast(I32))
+
+        def load_words(name, src, tag=None):
+            tile = sbuf(name, [P, 2 * H], U8, tag=tag)
+            nc.sync.dma_start(tile[:].bitcast(I32), src[0].bitcast(I32))
+            return tile
 
         def entries(tile, first, count):
             return tile[:, first // LANES : (first + count) // LANES]
 
-        xw = sb("xw", [P, T], I32)
-        xs = sb("xs", [P, T], U8)
-        raw_s = [sb("raw_s%d" % i, [P, H], U8) for i in range(3)]
-        gain_rows = sb("gain_rows", [P, P], F32)
-        ident = sb("ident", [P, P], F32)
-        warm = sb("warm", [P, 2], F32)
+        def deal_runs(engine, dst, src):
+            engine.tensor_copy(
+                dst[:].bitcast(I32).rearrange("p (t g r) -> p t g r", t=PACK, g=RUNS),
+                src[:].bitcast(I32).rearrange("p (g t r) -> p t g r", t=PACK, g=RUNS),
+            )
 
-        def load_words(i, src):
-            tile = sb("raw_w%d" % i, [P, 2 * H], U8, tag="raw_w")
-            nc.sync.dma_start(tile[:].bitcast(I32), src[0].bitcast(I32))
-            return tile
-
-        nc.vector.memset(xs[:].bitcast(I32), 0)
-        nc.gpsimd.memset(raw_s[0][:].bitcast(I32), 0)
-        load_scales(nc.gpsimd, raw_s[0], w1_scales)
-        nc.vector.memset(warm[:, 0:1], 0.0)
-        for i in (1, 2):
-            nc.vector.memset(raw_s[i][:].bitcast(I32), 0)
-        make_identity(nc, ident[:])
-        nc.gpsimd.memset(gain_rows[:], 0.0)
-
-        offs_t = load_list("offs_t", offs)
-        two_t = load_list("two_t", two)
-        nc.sync.dma_start(xw[:], x_words[0].rearrange("p n t -> p (n t)").bitcast(I32))
-        load_scales(nc.scalar, xs, x_scales)
-        raw_w = [load_words(0, w1_words)]
-        e0_t = load_list("e0_t", e0)
-        e1_t = load_list("e1_t", e1)
-        load_scales(nc.sync, raw_s[1], w2_scales)
-        nc.sync.dma_start(
-            gain_rows[0:PACK, :].rearrange("t (g r) -> t g r", r=LANES),
-            gn.rearrange("(g t r) o -> t g (r o)", t=PACK, r=LANES),
-        )
-        v0_t = load_list("v0_t", v0)
-        v1_t = load_list("v1_t", v1)
-        load_scales(nc.sync, raw_s[2], w3_scales)
-
-        nc.scalar.activation(warm[:, 1:2], warm[:, 0:1], ACT.Relu)
-
-        pick_s = [sb("pick_s%d" % i, [P, S], U8) for i in range(2)]
-        pick_w = [sb("pick_w%d" % i, [P, S], U32) for i in range(2)]
-        dealt_w = [sb("dealt_w%d" % i, [P, 2 * H], U8) for i in range(3)]
-        dealt_s = [sb("dealt_s%d" % i, [P, H], U8) for i in range(3)]
-
-        def deal_runs(i):
-            for dst, src in ((dealt_w[i], raw_w[i]), (dealt_s[i], raw_s[i])):
-                nc.gpsimd.tensor_copy(
-                    dst[:].bitcast(I32).rearrange("p (t g r) -> p t g r", t=PACK, g=8),
-                    src[:].bitcast(I32).rearrange("p (g t r) -> p t g r", t=PACK, g=8),
-                )
-
-        def project(i, dst, t, first, count):
+        def mx_product(dst, layer, t, codes, scales):
             nc.tensor.matmul_mx(
-                dst[:, first : first + count],
-                lhsT=dealt_w[i][:, 2 * P * t : 2 * P * (t + 1)].bitcast(FP4X4),
-                lhsT_scale=dealt_s[i][:, P * t : P * (t + 1)],
-                rhs=pick_w[i][:, first : first + count].bitcast(FP8X4),
-                rhs_scale=pick_s[i][:, first : first + count],
+                dst,
+                lhsT=dealt_words[layer][:, 2 * P * t : 2 * P * (t + 1)].bitcast(FP4X4),
+                lhsT_scale=dealt_scales[layer][:, P * t : P * (t + 1)],
+                rhs=codes[:].bitcast(FP8X4),
+                rhs_scale=scales[:],
                 start=True,
                 stop=True,
             )
 
-        nc.vector.tensor_copy(pick_s[0][:], xs[:].indirect(offs_t[:]))
-        nc.vector.tensor_copy(pick_s[1][:], xs[:].indirect(two_t[:]))
-        deal_runs(0)
-        raw_w.append(load_words(1, w2_words))
-        y_ps = [bank("y_ps%d" % t, "proj%d" % t) for t in range(PACK)]
-        for first in (0, HALF):
-            nc.vector.tensor_copy(
-                pick_w[0][:, first : first + HALF], xw[:].bitcast(U32).indirect(entries(offs_t, first, HALF))
-            )
-            for t in range(PACK):
-                project(0, y_ps[t], t, first, HALF)
-        y = [sb("y%d" % t, [P, S], F32) for t in range(PACK)]
+        x_table = sbuf("x_table", [P, T], I32)
+        x_scale_table = sbuf("x_scale_table", [P, T], U8)
+        w_scales = [sbuf("w_scales%d" % i, [P, H], U8) for i in range(3)]
+        gain_rows = sbuf("gain_rows", [P, P], F32)
+        ident = sbuf("ident", [P, P], F32)
+        zero = sbuf("zero", [P, 1], F32)
+        picked_scales = [sbuf("picked_scales%d" % i, [P, S], U8) for i in range(2)]
+        picked_words = [sbuf("picked_words%d" % i, [P, S], U32) for i in range(2)]
+        dealt_words = [sbuf("dealt_words%d" % i, [P, 2 * H], U8) for i in range(3)]
+        dealt_scales = [sbuf("dealt_scales%d" % i, [P, H], U8) for i in range(3)]
+
+        nc.gpsimd.memset(x_scale_table[:].bitcast(I32), 0)
+        nc.gpsimd.memset(w_scales[1][:].bitcast(I32), 0)
+        load_scales(nc.gpsimd, w_scales[1], w2_scales)
+        nc.vector.memset(zero[:], 0.0)
+        for i in (0, 2):
+            nc.vector.memset(w_scales[i][:].bitcast(I32), 0)
+        nc.scalar.activation(gain_rows[:], zero[:].to_broadcast([P, P]), ACT.Relu)
+        make_identity(nc, ident[:])
+
+        offs_list = load_list("offs_list", offs)
+        two_list = load_list("two_list", two)
+        w1_raw = load_words("w1_raw", w1_words)
+        load_scales(nc.sync, x_scale_table, x_scales)
+        nc.sync.dma_start(x_table[:], x_words[0].rearrange("p n t -> p (n t)").bitcast(I32))
+        load_scales(nc.sync, w_scales[0], w1_scales)
+        deal_runs(nc.vector, dealt_words[0], w1_raw)
+        deal_runs(nc.gpsimd, dealt_scales[0], w_scales[0])
+        e0_list = load_list("e0_list", e0)
+        e1_list = load_list("e1_list", e1)
+        w2_raw = load_words("w2_raw", w2_words, tag="w1_raw")
+        nc.sync.dma_start(
+            gain_rows[0:PACK, :].rearrange("t (g r) -> t g r", r=LANES),
+            gn.rearrange("(g t r) o -> t g (r o)", t=PACK, r=LANES),
+        )
+        w3_raw = load_words("w3_raw", w3_words)
+        load_scales(nc.sync, w_scales[2], w3_scales)
+        v0_list = load_list("v0_list", v0)
+        v1_list = load_list("v1_list", v1)
+
+        nc.vector.tensor_copy(picked_scales[0][:], x_scale_table[:].indirect(offs_list[:]))
+        nc.vector.tensor_copy(picked_scales[1][:], x_scale_table[:].indirect(two_list[:]))
+        y_banks = [bank("y_bank%d" % t, "plane%d" % t) for t in range(PACK)]
+        nc.vector.tensor_copy(picked_words[0][:], x_table[:].bitcast(U32).indirect(offs_list[:]))
         for t in range(PACK):
-            nc.scalar.copy(y[t][:], y_ps[t][:])
+            mx_product(y_banks[t][:], 0, t, picked_words[0], picked_scales[0])
+        y = [sbuf("y%d" % t, [P, S], F32) for t in range(PACK)]
+        for t in range(PACK):
+            nc.scalar.copy(y[t][:], y_banks[t][:])
 
-        nc.vector.tensor_copy(pick_w[1][:], xw[:].bitcast(U32).indirect(two_t[:]))
-        deal_runs(1)
-        raw_w.append(load_words(2, w3_words))
+        nc.vector.tensor_copy(picked_words[1][:], x_table[:].bitcast(U32).indirect(two_list[:]))
+        deal_runs(nc.vector, dealt_words[1], w2_raw)
+        deal_runs(nc.gpsimd, dealt_scales[1], w_scales[1])
+        nc.vector.tensor_copy(
+            dealt_words[2][:].rearrange("p (t m b) -> p t m b", t=PACK, b=2),
+            w3_raw[:].rearrange("p (m t b) -> p t m b", t=PACK, b=2),
+        )
 
-        gain_ps = bank("gain_ps", "pairs")
-        nc.tensor.transpose(gain_ps[:, 0:P], gain_rows[:], ident[:])
-        gain = sb("gain", [P, PACK], F32)
-        nc.scalar.copy(gain[:], gain_ps[:, 0:PACK])
+        gain_bank = bank("gain_bank", "pairs")
+        nc.tensor.transpose(gain_bank[:, 0:P], gain_rows[:], ident[:])
+        gain = sbuf("gain", [P, PACK], F32)
+        nc.scalar.copy(gain[:], gain_bank[:, 0:PACK])
 
-        rise, square, share0, share1 = {}, {}, {}, {}
+        c = [sbuf("c%d" % t, [P, S], F32) for t in range(PACK)]
+
+        def c_plane(t):
+            c_bank = bank("c_bank%d" % t, "plane%d" % t)
+            mx_product(c_bank[:], 1, t, picked_words[1], picked_scales[1])
+            nc.scalar.activation(c[t][:], c_bank[:], ACT.Copy, scale=gain[:, t : t + 1])
+
+        diff, rise, square, share0, share1 = {}, {}, {}, {}, {}
+        products, z_packed = {}, {}
 
         def flat(tile):
             return tile[:].rearrange("p t j -> p (t j)")
 
-        def differences(h, u):
-            step = 2 * h + u
-            low = sb("low%d" % step, [P, 2, HALF], F32, tag="work%d" % step)
-            diff = sb("diff%d" % step, [P, 2, HALF], F32)
-            fall = sb("fall%d" % step, [P, 2, HALF], F32)
-            rise[h, u] = sb("rise%d" % step, [P, 2, HALF], F32)
-            square[h, u] = sb("square%d" % step, [P, 2, HALF], F32, tag="work%d" % (step + 2))
+        def differences(quarter, buffer=None):
+            h, u = divmod(quarter, 2)
+            low = sbuf("low%d" % quarter, [P, 2, HALF], F32, tag=buffer)
+            diff[quarter] = sbuf("diff%d" % quarter, [P, 2, HALF], F32)
             for i in range(2):
-                nc.vector.tensor_copy(low[:, i, :], y[2 * u + i][:].indirect(entries(e0_t, HALF * h, HALF)))
+                nc.vector.tensor_copy(low[:, i, :], y[2 * u + i][:].indirect(entries(e0_list, HALF * h, HALF)))
             for i in range(2):
                 nc.vector.tensor_tensor(
-                    diff[:, i, :], y[2 * u + i][:].indirect(entries(e1_t, HALF * h, HALF)), low[:, i, :], ALU.subtract
+                    diff[quarter][:, i, :],
+                    y[2 * u + i][:].indirect(entries(e1_list, HALF * h, HALF)),
+                    low[:, i, :],
+                    ALU.subtract,
                 )
-            nc.scalar.activation(flat(rise[h, u]), flat(diff), ACT.Relu, bias=1.0)
-            nc.scalar.activation(flat(fall), flat(rise[h, u]), ACT.Relu, bias=2.0, scale=-1.0)
-            nc.scalar.activation(flat(square[h, u]), flat(fall), ACT.Square, scale=0.5)
 
-        def shares(h, u):
-            step = 2 * h + u
-            share0[h, u] = sb("share0_%d" % step, [P, 2, HALF], F32)
-            share1[h, u] = sb("share1_%d" % step, [P, 2, HALF], F32)
+        def steps(quarter):
+            rise[quarter] = sbuf("rise%d" % quarter, [P, 2, HALF], F32, tag="step%d" % quarter)
+            fall = sbuf("fall%d" % quarter, [P, 2, HALF], F32, tag="step%d" % (quarter + 1))
+            square[quarter] = sbuf("square%d" % quarter, [P, 2, HALF], F32)
+            for i in range(2):
+                nc.scalar.activation(rise[quarter][:, i, :], diff[quarter][:, i, :], ACT.Relu, bias=1.0)
+            for i in range(2):
+                nc.scalar.activation(fall[:, i, :], rise[quarter][:, i, :], ACT.Relu, bias=2.0, scale=-1.0)
+            for i in range(2):
+                nc.scalar.activation(square[quarter][:, i, :], fall[:, i, :], ACT.Square, scale=0.5)
+
+        def shares(quarter):
+            share0[quarter] = sbuf("share0_%d" % quarter, [P, 2, HALF], F32)
+            share1[quarter] = sbuf("share1_%d" % quarter, [P, 2, HALF], F32)
             nc.vector.scalar_tensor_tensor(
-                flat(share0[h, u]), flat(rise[h, u]), 1.0, flat(square[h, u]), ALU.add, ALU.mult
+                flat(share0[quarter]), flat(rise[quarter]), 1.0, flat(square[quarter]), ALU.add, ALU.mult
             )
-            nc.scalar.activation(flat(share1[h, u]), flat(share0[h, u]), ACT.Copy, bias=1.0, scale=-1.0)
+            nc.scalar.activation(flat(share1[quarter]), flat(share0[quarter]), ACT.Copy, bias=1.0, scale=-1.0)
 
-        c = [sb("c%d" % t, [P, S], F32) for t in range(PACK)]
+        def blend(b, plane_groups, buffer=None):
+            h, local = divmod(BLOCK * b, HALF)
+            for lo, hi in plane_groups:
+                tile = sbuf("products%d_%d" % (b, lo), [P, hi - lo, 2, BLOCK], F32, tag=buffer)
+                for t in range(lo, hi):
+                    products[b, t] = tile[:, t - lo, :, :]
+            for step in range(PACK + LEAD):
+                for i, t in ((1, step - LEAD), (0, step)):
+                    if 0 <= t < PACK:
+                        nc.vector.tensor_tensor(
+                            products[b, t][:, i, :],
+                            c[t][:].indirect(entries((v0_list, v1_list)[i], BLOCK * b, BLOCK)),
+                            (share0, share1)[i][2 * h + t // 2][:, t % 2, local : local + BLOCK],
+                            ALU.mult,
+                        )
 
-        def second_projection(t):
-            c_ps = bank("c_ps%d" % t, "proj%d" % t)
-            project(1, c_ps, t, 0, S)
-            nc.scalar.activation(c[t][:], c_ps[:], ACT.Copy, scale=gain[:, t : t + 1])
-
-        differences(0, 0)
-        second_projection(0)
-        differences(0, 1)
-        shares(0, 0)
-        second_projection(1)
-        differences(1, 0)
-        shares(0, 1)
-        second_projection(2)
-        second_projection(3)
-        differences(1, 1)
-
-        nc.vector.tensor_copy(
-            dealt_w[2][:].rearrange("p (t m b) -> p t m b", t=PACK, b=2),
-            raw_w[2][:].rearrange("p (m t b) -> p t m b", t=PACK, b=2),
-        )
-        nc.vector.tensor_copy(
-            dealt_s[2][:].rearrange("p (t m) -> p t m", t=PACK),
-            raw_s[2][:].rearrange("p (m t) -> p t m", t=PACK),
-        )
-
-        parts = {}
-        blocks = S // BLOCK
-        last = blocks - 1
-
-        def blend(b):
-            first = BLOCK * b
-            h, local = divmod(first, HALF)
-            for t in range(PACK):
-                for i, (lst, share) in enumerate(((v0_t, share0), (v1_t, share1))):
-                    parts[b, t, i] = sb("part%d_%d_%d" % (b, t, i), [P, BLOCK], F32)
-                    nc.vector.tensor_tensor(
-                        parts[b, t, i][:],
-                        c[t][:].indirect(entries(lst, first, BLOCK)),
-                        share[h, t // 2][:, t % 2, local : local + BLOCK],
-                        ALU.mult,
-                    )
-
-        out_codes = sb("out_codes", [P, S], U32)
-        out_scales = sb("out_scales", [P, S], U8)
-        out_rows = out_0.rearrange("(p t) j -> p t j", t=PACK)
-
-        z_packed = {}
-        o_packed = [sb("o_packed%d" % b, [P, BLOCK * PACK], BF16) for b in range(S // BLOCK)]
-
-        def turn(b):
-            z_rows = sb("z_rows%d" % b, [P, H], BF16, tag="z_rows")
-            successor = (b + 2, 0, 0) if b + 2 <= last else (last, PACK - 1, 0)
-            z_packed[b] = sb("z_packed%d" % b, [P, BLOCK * PACK], BF16, tag="part%d_%d_%d" % successor if b < last else None)
-            groups = ((0, PACK),) if b < last else ((0, PACK - 1), (PACK - 1, PACK))
-            for lo, hi in groups:
-                sums = bank("sums%d_%d" % (b, lo), "sums" if lo == 0 else "proj0")
+        def turn(b, plane_groups):
+            z_rows = sbuf("z_rows%d" % b, [P, H], BF16, tag="z_rows")
+            z_packed[b] = sbuf("z_packed%d" % b, [P, BLOCK * PACK], BF16)
+            for lo, hi in plane_groups:
+                sums = bank("sums%d_%d" % (b, lo), "sums" if lo == 0 else "plane0")
                 for t in range(lo, hi):
                     for i in range(2):
                         nc.tensor.matmul(
-                            sums[:, P * t : P * (t + 1)], lhsT=parts[b, t, i][:], rhs=ident[:],
+                            sums[:, P * t : P * (t + 1)], lhsT=products[b, t][:, i, :], rhs=ident[:],
                             is_transpose=True, start=i == 0, stop=i == 1,
                         )
-                nc.scalar.copy(
-                    z_rows[:].rearrange("j (g t r) -> j g t r", t=PACK, r=LANES)[:, :, lo:hi, :],
-                    sums[:].rearrange("j (t g r) -> j g t r", t=PACK, r=LANES)[:, :, lo:hi, :],
-                )
+                for u in range(2):
+                    nc.scalar.copy(
+                        z_rows[:].rearrange("j (u g t r e) -> j u g t r e", u=2, t=PACK, r=4, e=2)[:, u, :, lo:hi, :, :],
+                        sums[:].rearrange("j (t g r u e) -> j u g t r e", u=2, t=PACK, r=4, e=2)[:, u, :, lo:hi, :, :],
+                    )
             pairs = bank("pairs%d" % b, "pairs")
-            words = z_rows[:].bitcast(F32)
+            pair_words = z_rows[:].bitcast(F32)
             for u in range(2):
-                nc.tensor.transpose(pairs[:, BLOCK * u : BLOCK * (u + 1)], words[:, u : H // 2 : 2], ident[:])
+                nc.tensor.transpose(pairs[:, BLOCK * u : BLOCK * (u + 1)], pair_words[:, P * u : P * (u + 1)], ident[:])
             nc.scalar.copy(
                 z_packed[b][:].bitcast(F32).rearrange("p (j u) -> p j u", u=2),
                 pairs[:, 0 : 2 * BLOCK].rearrange("p (u j) -> p j u", u=2),
             )
 
-        def layer(b):
-            cols = slice(BLOCK * b, BLOCK * (b + 1))
-            z_codes = sb("z_codes%d" % b, [P, BLOCK], U32)
-            z_scales = sb("z_scales%d" % b, [P, BLOCK], U8)
-            nc.vector.quantize_mx(z_codes[:].bitcast(FP8X4), z_scales[:], z_packed[b][:])
-            result = sb("result%d" % b, [P, PACK, BLOCK], F32)
-            packed = o_packed[b][:].rearrange("p (j t) -> p j t", t=PACK)
-            groups = ((0, PACK),) if b < last else ((0, 2), (2, PACK))
-            for lo, hi in groups:
-                acc = bank("acc%d_%d" % (b, lo), "acc%d" % (b % 2) if lo == 0 else "proj1")
-                for t in range(lo, hi):
-                    nc.tensor.matmul_mx(
-                        acc[:, BLOCK * t : BLOCK * (t + 1)],
-                        lhsT=dealt_w[2][:, 2 * P * t : 2 * P * (t + 1)].bitcast(FP4X4),
-                        lhsT_scale=dealt_s[2][:, P * t : P * (t + 1)],
-                        rhs=z_codes[:].bitcast(FP8X4),
-                        rhs_scale=z_scales[:],
-                        start=True,
-                        stop=True,
-                    )
-                if b < last - 1:
-                    nc.scalar.copy(packed, acc[:].rearrange("p (t j) -> p j t", t=PACK))
-                copy = nc.vector.tensor_copy if (b == last - 1 or lo > 0) else nc.scalar.copy
-                copy(result[:, lo:hi, :].rearrange("p t j -> p (t j)"), acc[:, BLOCK * lo : BLOCK * hi])
-                nc.sync.dma_start(out_rows[:, lo:hi, cols], result[:, lo:hi, :])
-            if b >= last - 1:
-                nc.vector.tensor_copy(packed, result[:].rearrange("p t j -> p j t"))
-
-        def planes(b):
-            cols = slice(BLOCK * b, BLOCK * (b + 1))
-            nc.vector.quantize_mx(out_codes[:, cols].bitcast(FP8X4), out_scales[:, cols], o_packed[b][:])
-
+        out_codes = sbuf("out_codes", [P, S], U32)
+        out_scales = sbuf("out_scales", [P, S], U8)
+        out_packed = sbuf("out_packed", [P, S * PACK], BF16)
+        out_rows = out_0.rearrange("(p t) j -> p t j", t=PACK)
         out_words = out_1[0].rearrange("p n t -> p (n t)").bitcast(I32)
 
-        blend(0)
-        shares(1, 0)
-        turn(0)
-        blend(1)
-        shares(1, 1)
-        turn(1)
-        layer(0)
-        blend(2)
-        turn(2)
-        layer(1)
-        layer(2)
-        blend(3)
-        turn(3)
-        planes(0)
-        planes(1)
-        planes(2)
-        nc.sync.dma_start(out_words[:, 0 : BLOCK * last], out_codes[:, 0 : BLOCK * last].bitcast(I32))
-        layer(3)
-        planes(3)
+        def last_layer(b, row_groups, vector_is_free):
+            cols = slice(BLOCK * b, BLOCK * (b + 1))
+            z_codes = sbuf("z_codes%d" % b, [P, BLOCK], U32)
+            z_scales = sbuf("z_scales%d" % b, [P, BLOCK], U8)
+            nc.vector.quantize_mx(z_codes[:].bitcast(FP8X4), z_scales[:], z_packed[b][:])
+            result = sbuf("result%d" % b, [P, PACK, BLOCK], F32)
+            packed = out_packed[:].rearrange("p (j t) -> p j t", t=PACK)[:, cols, :]
+            for lo, hi in row_groups:
+                acc = bank("acc%d_%d" % (b, lo), "acc%d" % (b % 2) if lo == 0 else "plane1")
+                for t in range(lo, hi):
+                    mx_product(acc[:, BLOCK * t : BLOCK * (t + 1)], 2, t, z_codes, z_scales)
+                if not vector_is_free:
+                    nc.scalar.copy(packed, acc[:].rearrange("p (t j) -> p j t", t=PACK))
+                copy = nc.vector.tensor_copy if vector_is_free and hi == PACK else nc.scalar.copy
+                copy(result[:, lo:hi, :].rearrange("p t j -> p (t j)"), acc[:, BLOCK * lo : BLOCK * hi])
+                nc.sync.dma_start(out_rows[:, lo:hi, cols], result[:, lo:hi, :])
+            if vector_is_free:
+                nc.vector.tensor_copy(packed, result[:].rearrange("p t j -> p j t"))
 
-        nc.scalar.dma_start(out_words[:, BLOCK * last : S], out_codes[:, BLOCK * last : S].bitcast(I32))
-        for q in range(4):
-            queue = nc.scalar if q % 2 else nc.sync
-            queue.dma_start(
-                out_2[0, 4 * q : 4 * q + 4, :].bitcast(I32), out_scales[32 * q : 32 * q + 4, :].bitcast(I32)
+        def out_planes(first, count):
+            nc.vector.quantize_mx(
+                out_codes[:, first : first + count].bitcast(FP8X4),
+                out_scales[:, first : first + count],
+                out_packed[:, PACK * first : PACK * (first + count)],
             )
+
+        whole = ((0, PACK),)
+        halves = ((0, 2), (2, PACK))
+        short_end = ((0, PACK - 1), (PACK - 1, PACK))
+
+        c_plane(0)
+        c_plane(1)
+        differences(0)
+        steps(0)
+        c_plane(2)
+        c_plane(3)
+        differences(1)
+        steps(1)
+        nc.vector.tensor_copy(
+            dealt_scales[2][:].rearrange("p (t m) -> p t m", t=PACK),
+            w_scales[2][:].rearrange("p (m t) -> p t m", t=PACK),
+        )
+        differences(2)
+        shares(0)
+        shares(1)
+        steps(2)
+
+        blend(0, halves)
+        shares(2)
+        turn(0, whole)
+        differences(3, buffer="products0_0")
+        steps(3)
+        blend(1, whole, buffer="products0_0")
+        shares(3)
+        turn(1, whole)
+        last_layer(0, whole, vector_is_free=False)
+        blend(2, whole, buffer="z_packed0")
+        turn(2, whole)
+        last_layer(1, whole, vector_is_free=False)
+        blend(LAST, whole, buffer="z_packed1")
+
+        turn(LAST, short_end)
+        last_layer(2, whole, vector_is_free=True)
+        out_planes(0, HALF)
+        out_planes(HALF, BLOCK)
+        nc.sync.dma_start(out_words[:, 0 : BLOCK * LAST], out_codes[:, 0 : BLOCK * LAST].bitcast(I32))
+        last_layer(LAST, halves, vector_is_free=True)
+        out_planes(BLOCK * LAST, BLOCK)
+
+        nc.scalar.dma_start(out_words[:, BLOCK * LAST : S], out_codes[:, BLOCK * LAST : S].bitcast(I32))
+        for q in range(QUADRANTS):
+            queue = nc.scalar if q % 2 else nc.sync
+            queue.dma_start(out_2[0, PACK * q : PACK * (q + 1), :].bitcast(I32), scale_rows(out_scales, q))

from contextlib import ExitStack

import concourse.mybir as mybir
from concourse.masks import make_identity

K, T, S, N, H = 512, 2048, 512, 512, 512
FLOPS = 2 * K * H * S * 2 + 2 * H * N * S

F32 = mybir.dt.float32
BF16 = mybir.dt.bfloat16
I32 = mybir.dt.int32
U32 = mybir.dt.uint32
U16 = mybir.dt.uint16
U8 = mybir.dt.uint8
FP8X4 = mybir.dt.float8_e4m3fn_x4
FP4X4 = mybir.dt.float4_e2m1fn_x4
ACT = mybir.ActivationFunctionType
ALU = mybir.AluOpType

P = 128
PACK = 4
LANES = 16
RUNS = P // LANES
QUADRANTS = 4
HALF = S // 2
BLOCK = 128
BLOCKS = S // BLOCK
LAST = BLOCKS - 1
LEAD = 2


def tile_picked_smstep_none_po_kernel(
    tc, x_words, x_scales, w1_words, w1_scales, w2_words, w2_scales, gn, w3_words, w3_scales,
    offs, two, e1, e0, v0, v1, out_0, out_1, out_2,
):
    nc = tc.nc
    with ExitStack() as ctx:
        keep = ctx.enter_context(tc.tile_pool(name="keep", bufs=1))
        psum = ctx.enter_context(tc.psum_pool(name="psum", bufs=1))

        def sbuf(name, shape, dtype, tag=None):
            return keep.tile(shape, dtype, name=name, tag=tag or name, align_bytes=64)

        def bank(name, tag):
            return psum.tile([P, PACK * BLOCK], F32, name=name, tag=tag)

        def load_list(name, src):
            tile = sbuf(name, [P, S // LANES], U16)
            nc.sync.dma_start(tile[:], src)
            return tile

        def scale_rows(tile, q):
            return tile[32 * q : 32 * q + PACK, :].bitcast(I32)

        def load_scales(queue, tile, src):
            for q in range(QUADRANTS):
                queue.dma_start(scale_rows(tile, q), src[0, PACK * q : PACK * (q + 1), :].bitcast(I32))

        def load_words(name, src, tag=None):
            tile = sbuf(name, [P, 2 * H], U8, tag=tag)
            nc.sync.dma_start(tile[:].bitcast(I32), src[0].bitcast(I32))
            return tile

        def entries(tile, first, count):
            return tile[:, first // LANES : (first + count) // LANES]

        def deal_runs(engine, dst, src):
            engine.tensor_copy(
                dst[:].bitcast(I32).rearrange("p (t g r) -> p t g r", t=PACK, g=RUNS),
                src[:].bitcast(I32).rearrange("p (g t r) -> p t g r", t=PACK, g=RUNS),
            )

        def mx_product(dst, layer, t, codes, scales):
            nc.tensor.matmul_mx(
                dst,
                lhsT=dealt_words[layer][:, 2 * P * t : 2 * P * (t + 1)].bitcast(FP4X4),
                lhsT_scale=dealt_scales[layer][:, P * t : P * (t + 1)],
                rhs=codes[:].bitcast(FP8X4),
                rhs_scale=scales[:],
                start=True,
                stop=True,
            )

        x_table = sbuf("x_table", [P, T], I32)
        x_scale_table = sbuf("x_scale_table", [P, T], U8)
        w_scales = [sbuf("w_scales%d" % i, [P, H], U8) for i in range(3)]
        gain_rows = sbuf("gain_rows", [P, P], F32)
        ident = sbuf("ident", [P, P], F32)
        zero = sbuf("zero", [P, 1], F32)
        picked_scales = [sbuf("picked_scales%d" % i, [P, S], U8) for i in range(2)]
        picked_words = [sbuf("picked_words%d" % i, [P, S], U32) for i in range(2)]
        dealt_words = [sbuf("dealt_words%d" % i, [P, 2 * H], U8) for i in range(3)]
        dealt_scales = [sbuf("dealt_scales%d" % i, [P, H], U8) for i in range(3)]

        nc.gpsimd.memset(x_scale_table[:].bitcast(I32), 0)
        nc.gpsimd.memset(w_scales[1][:].bitcast(I32), 0)
        load_scales(nc.gpsimd, w_scales[1], w2_scales)
        nc.vector.memset(zero[:], 0.0)
        for i in (0, 2):
            nc.vector.memset(w_scales[i][:].bitcast(I32), 0)
        nc.scalar.activation(gain_rows[:], zero[:].to_broadcast([P, P]), ACT.Relu)
        make_identity(nc, ident[:])

        offs_list = load_list("offs_list", offs)
        two_list = load_list("two_list", two)
        w1_raw = load_words("w1_raw", w1_words)
        load_scales(nc.sync, x_scale_table, x_scales)
        nc.sync.dma_start(x_table[:], x_words[0].rearrange("p n t -> p (n t)").bitcast(I32))
        load_scales(nc.sync, w_scales[0], w1_scales)
        deal_runs(nc.vector, dealt_words[0], w1_raw)
        deal_runs(nc.gpsimd, dealt_scales[0], w_scales[0])
        e0_list = load_list("e0_list", e0)
        e1_list = load_list("e1_list", e1)
        w2_raw = load_words("w2_raw", w2_words, tag="w1_raw")
        nc.sync.dma_start(
            gain_rows[0:PACK, :].rearrange("t (g r) -> t g r", r=LANES),
            gn.rearrange("(g t r) o -> t g (r o)", t=PACK, r=LANES),
        )
        w3_raw = load_words("w3_raw", w3_words)
        load_scales(nc.sync, w_scales[2], w3_scales)
        v0_list = load_list("v0_list", v0)
        v1_list = load_list("v1_list", v1)

        nc.vector.tensor_copy(picked_scales[0][:], x_scale_table[:].indirect(offs_list[:]))
        nc.vector.tensor_copy(picked_scales[1][:], x_scale_table[:].indirect(two_list[:]))
        y_banks = [bank("y_bank%d" % t, "plane%d" % t) for t in range(PACK)]
        nc.vector.tensor_copy(picked_words[0][:], x_table[:].bitcast(U32).indirect(offs_list[:]))
        for t in range(PACK):
            mx_product(y_banks[t][:], 0, t, picked_words[0], picked_scales[0])
        y = [sbuf("y%d" % t, [P, S], F32) for t in range(PACK)]
        for t in range(PACK):
            nc.scalar.copy(y[t][:], y_banks[t][:])

        nc.vector.tensor_copy(picked_words[1][:], x_table[:].bitcast(U32).indirect(two_list[:]))
        deal_runs(nc.vector, dealt_words[1], w2_raw)
        deal_runs(nc.gpsimd, dealt_scales[1], w_scales[1])
        nc.vector.tensor_copy(
            dealt_words[2][:].rearrange("p (t m b) -> p t m b", t=PACK, b=2),
            w3_raw[:].rearrange("p (m t b) -> p t m b", t=PACK, b=2),
        )

        gain_bank = bank("gain_bank", "pairs")
        nc.tensor.transpose(gain_bank[:, 0:P], gain_rows[:], ident[:])
        gain = sbuf("gain", [P, PACK], F32)
        nc.scalar.copy(gain[:], gain_bank[:, 0:PACK])

        c = [sbuf("c%d" % t, [P, S], F32) for t in range(PACK)]

        def c_plane(t):
            c_bank = bank("c_bank%d" % t, "plane%d" % t)
            mx_product(c_bank[:], 1, t, picked_words[1], picked_scales[1])
            nc.scalar.activation(c[t][:], c_bank[:], ACT.Copy, scale=gain[:, t : t + 1])

        diff, rise, square, share0, share1 = {}, {}, {}, {}, {}
        products, z_packed = {}, {}

        def flat(tile):
            return tile[:].rearrange("p t j -> p (t j)")

        def differences(quarter, buffer=None):
            h, u = divmod(quarter, 2)
            low = sbuf("low%d" % quarter, [P, 2, HALF], F32, tag=buffer)
            diff[quarter] = sbuf("diff%d" % quarter, [P, 2, HALF], F32)
            for i in range(2):
                nc.vector.tensor_copy(low[:, i, :], y[2 * u + i][:].indirect(entries(e0_list, HALF * h, HALF)))
            for i in range(2):
                nc.vector.tensor_tensor(
                    diff[quarter][:, i, :],
                    y[2 * u + i][:].indirect(entries(e1_list, HALF * h, HALF)),
                    low[:, i, :],
                    ALU.subtract,
                )

        def steps(quarter):
            rise[quarter] = sbuf("rise%d" % quarter, [P, 2, HALF], F32, tag="step%d" % quarter)
            fall = sbuf("fall%d" % quarter, [P, 2, HALF], F32, tag="step%d" % (quarter + 1))
            square[quarter] = sbuf("square%d" % quarter, [P, 2, HALF], F32)
            for i in range(2):
                nc.scalar.activation(rise[quarter][:, i, :], diff[quarter][:, i, :], ACT.Relu, bias=1.0)
            for i in range(2):
                nc.scalar.activation(fall[:, i, :], rise[quarter][:, i, :], ACT.Relu, bias=2.0, scale=-1.0)
            for i in range(2):
                nc.scalar.activation(square[quarter][:, i, :], fall[:, i, :], ACT.Square, scale=0.5)

        def shares(quarter):
            share0[quarter] = sbuf("share0_%d" % quarter, [P, 2, HALF], F32)
            share1[quarter] = sbuf("share1_%d" % quarter, [P, 2, HALF], F32)
            nc.vector.scalar_tensor_tensor(
                flat(share0[quarter]), flat(rise[quarter]), 1.0, flat(square[quarter]), ALU.add, ALU.mult
            )
            nc.scalar.activation(flat(share1[quarter]), flat(share0[quarter]), ACT.Copy, bias=1.0, scale=-1.0)

        def blend(b, plane_groups, buffer=None):
            h, local = divmod(BLOCK * b, HALF)
            for lo, hi in plane_groups:
                tile = sbuf("products%d_%d" % (b, lo), [P, hi - lo, 2, BLOCK], F32, tag=buffer)
                for t in range(lo, hi):
                    products[b, t] = tile[:, t - lo, :, :]
            for step in range(PACK + LEAD):
                for i, t in ((1, step - LEAD), (0, step)):
                    if 0 <= t < PACK:
                        nc.vector.tensor_tensor(
                            products[b, t][:, i, :],
                            c[t][:].indirect(entries((v0_list, v1_list)[i], BLOCK * b, BLOCK)),
                            (share0, share1)[i][2 * h + t // 2][:, t % 2, local : local + BLOCK],
                            ALU.mult,
                        )

        def turn(b, plane_groups):
            z_rows = sbuf("z_rows%d" % b, [P, H], BF16, tag="z_rows")
            z_packed[b] = sbuf("z_packed%d" % b, [P, BLOCK * PACK], BF16)
            for lo, hi in plane_groups:
                sums = bank("sums%d_%d" % (b, lo), "sums" if lo == 0 else "plane0")
                for t in range(lo, hi):
                    for i in range(2):
                        nc.tensor.matmul(
                            sums[:, P * t : P * (t + 1)], lhsT=products[b, t][:, i, :], rhs=ident[:],
                            is_transpose=True, start=i == 0, stop=i == 1,
                        )
                for u in range(2):
                    nc.scalar.copy(
                        z_rows[:].rearrange("j (u g t r e) -> j u g t r e", u=2, t=PACK, r=4, e=2)[:, u, :, lo:hi, :, :],
                        sums[:].rearrange("j (t g r u e) -> j u g t r e", u=2, t=PACK, r=4, e=2)[:, u, :, lo:hi, :, :],
                    )
            pairs = bank("pairs%d" % b, "pairs")
            pair_words = z_rows[:].bitcast(F32)
            for u in range(2):
                nc.tensor.transpose(pairs[:, BLOCK * u : BLOCK * (u + 1)], pair_words[:, P * u : P * (u + 1)], ident[:])
            nc.scalar.copy(
                z_packed[b][:].bitcast(F32).rearrange("p (j u) -> p j u", u=2),
                pairs[:, 0 : 2 * BLOCK].rearrange("p (u j) -> p j u", u=2),
            )

        out_codes = sbuf("out_codes", [P, S], U32)
        out_scales = sbuf("out_scales", [P, S], U8)
        out_packed = sbuf("out_packed", [P, S * PACK], BF16)
        out_rows = out_0.rearrange("(p t) j -> p t j", t=PACK)
        out_words = out_1[0].rearrange("p n t -> p (n t)").bitcast(I32)

        def last_layer(b, row_groups, vector_is_free):
            cols = slice(BLOCK * b, BLOCK * (b + 1))
            z_codes = sbuf("z_codes%d" % b, [P, BLOCK], U32)
            z_scales = sbuf("z_scales%d" % b, [P, BLOCK], U8)
            nc.vector.quantize_mx(z_codes[:].bitcast(FP8X4), z_scales[:], z_packed[b][:])
            result = sbuf("result%d" % b, [P, PACK, BLOCK], F32)
            packed = out_packed[:].rearrange("p (j t) -> p j t", t=PACK)[:, cols, :]
            for lo, hi in row_groups:
                acc = bank("acc%d_%d" % (b, lo), "acc%d" % (b % 2) if lo == 0 else "plane1")
                for t in range(lo, hi):
                    mx_product(acc[:, BLOCK * t : BLOCK * (t + 1)], 2, t, z_codes, z_scales)
                if not vector_is_free:
                    nc.scalar.copy(packed, acc[:].rearrange("p (t j) -> p j t", t=PACK))
                copy = nc.vector.tensor_copy if vector_is_free and hi == PACK else nc.scalar.copy
                copy(result[:, lo:hi, :].rearrange("p t j -> p (t j)"), acc[:, BLOCK * lo : BLOCK * hi])
                nc.sync.dma_start(out_rows[:, lo:hi, cols], result[:, lo:hi, :])
            if vector_is_free:
                nc.vector.tensor_copy(packed, result[:].rearrange("p t j -> p j t"))

        def out_planes(first, count):
            nc.vector.quantize_mx(
                out_codes[:, first : first + count].bitcast(FP8X4),
                out_scales[:, first : first + count],
                out_packed[:, PACK * first : PACK * (first + count)],
            )

        whole = ((0, PACK),)
        halves = ((0, 2), (2, PACK))
        short_end = ((0, PACK - 1), (PACK - 1, PACK))

        c_plane(0)
        c_plane(1)
        differences(0)
        steps(0)
        c_plane(2)
        c_plane(3)
        differences(1)
        steps(1)
        nc.vector.tensor_copy(
            dealt_scales[2][:].rearrange("p (t m) -> p t m", t=PACK),
            w_scales[2][:].rearrange("p (m t) -> p t m", t=PACK),
        )
        differences(2)
        shares(0)
        shares(1)
        steps(2)

        blend(0, halves)
        shares(2)
        turn(0, whole)
        differences(3, buffer="products0_0")
        steps(3)
        blend(1, whole, buffer="products0_0")
        shares(3)
        turn(1, whole)
        last_layer(0, whole, vector_is_free=False)
        blend(2, whole, buffer="z_packed0")
        turn(2, whole)
        last_layer(1, whole, vector_is_free=False)
        blend(LAST, whole, buffer="z_packed1")

        turn(LAST, short_end)
        last_layer(2, whole, vector_is_free=True)
        out_planes(0, HALF)
        out_planes(HALF, BLOCK)
        nc.sync.dma_start(out_words[:, 0 : BLOCK * LAST], out_codes[:, 0 : BLOCK * LAST].bitcast(I32))
        last_layer(LAST, halves, vector_is_free=True)
        out_planes(BLOCK * LAST, BLOCK)

        nc.scalar.dma_start(out_words[:, BLOCK * LAST : S], out_codes[:, BLOCK * LAST : S].bitcast(I32))
        for q in range(QUADRANTS):
            queue = nc.scalar if q % 2 else nc.sync
            queue.dma_start(out_2[0, PACK * q : PACK * (q + 1), :].bitcast(I32), scale_rows(out_scales, q))
